import numpy as np
import ml_dtypes

BF16 = ml_dtypes.bfloat16


def bf(x):
    return np.asarray(x, np.float32).astype(BF16)


def f32(x):
    return np.asarray(x, np.float32)


def f64(x):
    return np.asarray(x).astype(np.float64)


def striped(idx):
    return np.tile(idx.reshape(-1, 16).T, (8, 1))


S, K, M, N, E, Q = 2048, 128, 128, 4096, 8, 512


def two_experts():
    first = np.random.permutation(S).reshape(E, S // E)
    return np.concatenate([np.random.permutation(np.concatenate([first[e], first[(e + 1) % E]])) for e in range(E)])


def setup_inputs():
    return {"table": bf(np.random.standard_normal((K, S))), "w": bf(np.random.standard_normal((E, K, M)) / np.sqrt(K)), "b": f32(0.5 * np.random.standard_normal((M, 1))), "offs": striped(two_experts())}


def reference(table, w, b, offs):
    idx = offs[:16].T.reshape(-1)
    x = f64(table)[:, idx]
    y = np.concatenate([f64(w)[e].T @ x[:, e * Q : (e + 1) * Q] for e in range(E)], axis=1)
    return np.maximum(y + f64(b), 0.0)

@@ -1,0 +1,45 @@
+import concourse.mybir as mybir
+
+BF16, F32, U16 = mybir.dt.bfloat16, mybir.dt.float32, mybir.dt.uint16
+RELU = mybir.ActivationFunctionType.Relu
+ADD, MAX = mybir.AluOpType.add, mybir.AluOpType.max
+
+P = 128
+TOKENS = 2048
+EXPERTS = 8
+PIECE = 512
+LIST = EXPERTS * PIECE
+PIECE_COLS = PIECE // 16
+
+FLOPS = 2 * P * P * LIST
+
+
+def tile_gather_matmul_kernel(tc, table, w, b, offs, out):
+    nc = tc.nc
+    with (
+        tc.tile_pool(name="held", bufs=1) as held,
+        tc.tile_pool(name="staged", bufs=EXPERTS) as staged,
+        tc.psum_pool(name="psum", bufs=EXPERTS) as psum,
+    ):
+        offsets = held.tile([P, LIST // 16], U16, name="offsets")
+        nc.sync.dma_start(offsets[:], offs)
+        tokens = held.tile([P, TOKENS], BF16, name="tokens")
+        nc.scalar.dma_start(tokens[:], table)
+        weights = held.tile([P, EXPERTS, P], BF16, name="weights")
+        nc.gpsimd.dma_start(weights[:], w.rearrange("e k m -> k e m"))
+        bias = held.tile([P, 1], F32, name="bias")
+        nc.sync.dma_start(bias[:], b)
+
+        for e in range(EXPERTS):
+            bank = psum.tile([P, PIECE], F32, name="bank")
+            picked = tokens[:].indirect(offsets[:, e * PIECE_COLS : (e + 1) * PIECE_COLS])
+            nc.tensor.matmul(bank[:], weights[:, e, :], picked, start=True, stop=True)
+
+            layer = staged.tile([P, PIECE], F32, name="layer")
+            columns = out[:, e * PIECE : (e + 1) * PIECE]
+            if e % 2 == 0:
+                nc.scalar.activation(layer[:], bank[:], RELU, bias=bias[:])
+                nc.scalar.dma_start(columns, layer[:])
+            else:
+                nc.vector.tensor_scalar(layer[:], bank[:], bias[:], 0.0, op0=ADD, op1=MAX)
+                nc.sync.dma_start(columns, layer[:])

@@ -9,7 +9,9 @@ TOKENS = 2048
 EXPERTS = 8
 PIECE = 512
 LIST = EXPERTS * PIECE
-PIECE_COLS = PIECE // 16
+HALF = PIECE // 2
+BANKS = 8
+WARM_UP = 4
 
 FLOPS = 2 * P * P * LIST
 
@@ -18,28 +20,41 @@ def tile_gather_matmul_kernel(tc, table, w, b, offs, out):
     nc = tc.nc
     with (
         tc.tile_pool(name="held", bufs=1) as held,
-        tc.tile_pool(name="staged", bufs=EXPERTS) as staged,
-        tc.psum_pool(name="psum", bufs=EXPERTS) as psum,
+        tc.tile_pool(name="staged", bufs=2 * EXPERTS) as staged,
+        tc.psum_pool(name="psum", bufs=BANKS) as psum,
     ):
         offsets = held.tile([P, LIST // 16], U16, name="offsets")
         nc.sync.dma_start(offsets[:], offs)
+        weights = [held.tile([P, P], BF16, name=f"weights{e}") for e in range(EXPERTS)]
+        nc.scalar.dma_start(weights[0][:], w[0])
         tokens = held.tile([P, TOKENS], BF16, name="tokens")
-        nc.scalar.dma_start(tokens[:], table)
-        weights = held.tile([P, EXPERTS, P], BF16, name="weights")
-        nc.gpsimd.dma_start(weights[:], w.rearrange("e k m -> k e m"))
+        middle = TOKENS // 2
+        nc.sync.dma_start(tokens[:, :middle], table[:, :middle])
+        nc.scalar.dma_start(tokens[:, middle:], table[:, middle:])
         bias = held.tile([P, 1], F32, name="bias")
-        nc.sync.dma_start(bias[:], b)
+        nc.gpsimd.dma_start(bias[:], b)
+        for e in range(1, EXPERTS):
+            nc.sync.dma_start(weights[e][:], w[e])
+
+        zeros = held.tile([P, PIECE], BF16, name="zeros")
+        nc.vector.memset(zeros[:], 0.0)
+        unread = psum.tile([P, PIECE], F32, name="bank")
+        for _ in range(WARM_UP):
+            nc.tensor.matmul(unread[:], zeros[:, :P], zeros[:], start=True, stop=True)
+        first_relu = held.tile([P, 1], F32, name="first_relu")
+        nc.scalar.activation(first_relu[:], zeros[:, :1], RELU)
 
         for e in range(EXPERTS):
-            bank = psum.tile([P, PIECE], F32, name="bank")
-            picked = tokens[:].indirect(offsets[:, e * PIECE_COLS : (e + 1) * PIECE_COLS])
-            nc.tensor.matmul(bank[:], weights[:, e, :], picked, start=True, stop=True)
-
-            layer = staged.tile([P, PIECE], F32, name="layer")
-            columns = out[:, e * PIECE : (e + 1) * PIECE]
-            if e % 2 == 0:
-                nc.scalar.activation(layer[:], bank[:], RELU, bias=bias[:])
-                nc.scalar.dma_start(columns, layer[:])
-            else:
-                nc.vector.tensor_scalar(layer[:], bank[:], bias[:], 0.0, op0=ADD, op1=MAX)
-                nc.sync.dma_start(columns, layer[:])
+            for side in range(2):
+                first = e * PIECE + side * HALF
+                bank = psum.tile([P, HALF], F32, name="bank")
+                picked = tokens[:].indirect(offsets[:, first // 16 : (first + HALF) // 16])
+                nc.tensor.matmul(bank[:], weights[e][:], picked, start=True, stop=True)
+                layer = staged.tile([P, HALF], F32, name="layer")
+                columns = out[:, first : first + HALF]
+                if side == 0:
+                    nc.scalar.activation(layer[:], bank[:], RELU, bias=bias[:])
+                    nc.scalar.dma_start(columns, layer[:])
+                else:
+                    nc.vector.tensor_scalar(layer[:], bank[:], bias[:], 0.0, op0=ADD, op1=MAX)
+                    nc.sync.dma_start(columns, layer[:])

@@ -20,7 +20,7 @@ def tile_gather_matmul_kernel(tc, table, w, b, offs, out):
     nc = tc.nc
     with (
         tc.tile_pool(name="held", bufs=1) as held,
-        tc.tile_pool(name="staged", bufs=2 * EXPERTS) as staged,
+        tc.tile_pool(name="staged", bufs=EXPERTS) as staged,
         tc.psum_pool(name="psum", bufs=BANKS) as psum,
     ):
         offsets = held.tile([P, LIST // 16], U16, name="offsets")
@@ -45,16 +45,14 @@ def tile_gather_matmul_kernel(tc, table, w, b, offs, out):
         nc.scalar.activation(first_relu[:], zeros[:, :1], RELU)
 
         for e in range(EXPERTS):
+            layer = staged.tile([P, PIECE], F32, name="layer")
             for side in range(2):
                 first = e * PIECE + side * HALF
                 bank = psum.tile([P, HALF], F32, name="bank")
                 picked = tokens[:].indirect(offsets[:, first // 16 : (first + HALF) // 16])
                 nc.tensor.matmul(bank[:], weights[e][:], picked, start=True, stop=True)
-                layer = staged.tile([P, HALF], F32, name="layer")
-                columns = out[:, first : first + HALF]
                 if side == 0:
-                    nc.scalar.activation(layer[:], bank[:], RELU, bias=bias[:])
-                    nc.scalar.dma_start(columns, layer[:])
+                    nc.scalar.activation(layer[:, :HALF], bank[:], RELU, bias=bias[:])
                 else:
-                    nc.vector.tensor_scalar(layer[:], bank[:], bias[:], 0.0, op0=ADD, op1=MAX)
-                    nc.sync.dma_start(columns, layer[:])
+                    nc.vector.tensor_scalar(layer[:, HALF:], bank[:], bias[:], 0.0, op0=ADD, op1=MAX)
+            nc.sync.dma_start(out[:, e * PIECE : (e + 1) * PIECE], layer[:])

@@ -11,7 +11,6 @@ PIECE = 512
 LIST = EXPERTS * PIECE
 HALF = PIECE // 2
 BANKS = 8
-WARM_UP = 4
 
 FLOPS = 2 * P * P * LIST
 
@@ -36,13 +35,10 @@ def tile_gather_matmul_kernel(tc, table, w, b, offs, out):
         for e in range(1, EXPERTS):
             nc.sync.dma_start(weights[e][:], w[e])
 
-        zeros = held.tile([P, PIECE], BF16, name="zeros")
+        zeros = held.tile([P, 1], F32, name="zeros")
         nc.vector.memset(zeros[:], 0.0)
-        unread = psum.tile([P, PIECE], F32, name="bank")
-        for _ in range(WARM_UP):
-            nc.tensor.matmul(unread[:], zeros[:, :P], zeros[:], start=True, stop=True)
         first_relu = held.tile([P, 1], F32, name="first_relu")
-        nc.scalar.activation(first_relu[:], zeros[:, :1], RELU)
+        nc.scalar.activation(first_relu[:], zeros[:], RELU)
 
         for e in range(EXPERTS):
             layer = staged.tile([P, PIECE], F32, name="layer")

@@ -31,7 +31,7 @@ def tile_gather_matmul_kernel(tc, table, w, b, offs, out):
         nc.sync.dma_start(tokens[:, :middle], table[:, :middle])
         nc.scalar.dma_start(tokens[:, middle:], table[:, middle:])
         bias = held.tile([P, 1], F32, name="bias")
-        nc.gpsimd.dma_start(bias[:], b)
+        nc.sync.dma_start(bias[:], b)
         for e in range(1, EXPERTS):
             nc.sync.dma_start(weights[e][:], w[e])
 

@@ -25,11 +25,9 @@ def tile_gather_matmul_kernel(tc, table, w, b, offs, out):
         offsets = held.tile([P, LIST // 16], U16, name="offsets")
         nc.sync.dma_start(offsets[:], offs)
         weights = [held.tile([P, P], BF16, name=f"weights{e}") for e in range(EXPERTS)]
-        nc.scalar.dma_start(weights[0][:], w[0])
+        nc.sync.dma_start(weights[0][:], w[0])
         tokens = held.tile([P, TOKENS], BF16, name="tokens")
-        middle = TOKENS // 2
-        nc.sync.dma_start(tokens[:, :middle], table[:, :middle])
-        nc.scalar.dma_start(tokens[:, middle:], table[:, middle:])
+        nc.scalar.dma_start(tokens[:], table)
         bias = held.tile([P, 1], F32, name="bias")
         nc.sync.dma_start(bias[:], b)
         for e in range(1, EXPERTS):

@@ -9,7 +9,7 @@ TOKENS = 2048
 EXPERTS = 8
 PIECE = 512
 LIST = EXPERTS * PIECE
-HALF = PIECE // 2
+WIDE = 352
 BANKS = 8
 
 FLOPS = 2 * P * P * LIST
@@ -40,13 +40,12 @@ def tile_gather_matmul_kernel(tc, table, w, b, offs, out):
 
         for e in range(EXPERTS):
             layer = staged.tile([P, PIECE], F32, name="layer")
-            for side in range(2):
-                first = e * PIECE + side * HALF
-                bank = psum.tile([P, HALF], F32, name="bank")
-                picked = tokens[:].indirect(offsets[:, first // 16 : (first + HALF) // 16])
-                nc.tensor.matmul(bank[:], weights[e][:], picked, start=True, stop=True)
-                if side == 0:
-                    nc.scalar.activation(layer[:, :HALF], bank[:], RELU, bias=bias[:])
+            for lo, hi in ((0, WIDE), (WIDE, PIECE)):
+                bank = psum.tile([P, hi - lo], F32, name="bank")
+                entries = offsets[:, (e * PIECE + lo) // 16 : (e * PIECE + hi) // 16]
+                nc.tensor.matmul(bank[:], weights[e][:], tokens[:].indirect(entries), start=True, stop=True)
+                if lo == 0:
+                    nc.scalar.activation(layer[:, lo:hi], bank[:], RELU, bias=bias[:])
                 else:
-                    nc.vector.tensor_scalar(layer[:, HALF:], bank[:], bias[:], 0.0, op0=ADD, op1=MAX)
+                    nc.vector.tensor_scalar(layer[:, lo:hi], bank[:], bias[:], 0.0, op0=ADD, op1=MAX)
             nc.sync.dma_start(out[:, e * PIECE : (e + 1) * PIECE], layer[:])

@@ -11,6 +11,7 @@ PIECE = 512
 LIST = EXPERTS * PIECE
 WIDE = 352
 BANKS = 8
+ROW_START = 256
 
 FLOPS = 2 * P * P * LIST
 
@@ -22,11 +23,11 @@ def tile_gather_matmul_kernel(tc, table, w, b, offs, out):
         tc.tile_pool(name="staged", bufs=EXPERTS) as staged,
         tc.psum_pool(name="psum", bufs=BANKS) as psum,
     ):
-        offsets = held.tile([P, LIST // 16], U16, name="offsets")
+        offsets = held.tile([P, LIST // 16], U16, name="offsets", align_bytes=ROW_START)
         nc.sync.dma_start(offsets[:], offs)
-        weights = [held.tile([P, P], BF16, name=f"weights{e}") for e in range(EXPERTS)]
+        weights = [held.tile([P, P], BF16, name=f"weights{e}", align_bytes=ROW_START) for e in range(EXPERTS)]
         nc.sync.dma_start(weights[0][:], w[0])
-        tokens = held.tile([P, TOKENS], BF16, name="tokens")
+        tokens = held.tile([P, TOKENS], BF16, name="tokens", align_bytes=ROW_START)
         nc.scalar.dma_start(tokens[:], table)
         bias = held.tile([P, 1], F32, name="bias")
         nc.sync.dma_start(bias[:], b)
@@ -39,7 +40,7 @@ def tile_gather_matmul_kernel(tc, table, w, b, offs, out):
         nc.scalar.activation(first_relu[:], zeros[:], RELU)
 
         for e in range(EXPERTS):
-            layer = staged.tile([P, PIECE], F32, name="layer")
+            layer = staged.tile([P, PIECE], F32, name="layer", align_bytes=ROW_START)
             for lo, hi in ((0, WIDE), (WIDE, PIECE)):
                 bank = psum.tile([P, hi - lo], F32, name="bank")
                 entries = offsets[:, (e * PIECE + lo) // 16 : (e * PIECE + hi) // 16]

@@ -10,6 +10,7 @@ EXPERTS = 8
 PIECE = 512
 LIST = EXPERTS * PIECE
 WIDE = 352
+HALF = PIECE // 2
 BANKS = 8
 ROW_START = 256
 
@@ -40,8 +41,10 @@ def tile_gather_matmul_kernel(tc, table, w, b, offs, out):
         nc.scalar.activation(first_relu[:], zeros[:], RELU)
 
         for e in range(EXPERTS):
+            last = e == EXPERTS - 1
+            cut = HALF if last else WIDE
             layer = staged.tile([P, PIECE], F32, name="layer", align_bytes=ROW_START)
-            for lo, hi in ((0, WIDE), (WIDE, PIECE)):
+            for lo, hi in ((0, cut), (cut, PIECE)):
                 bank = psum.tile([P, hi - lo], F32, name="bank")
                 entries = offsets[:, (e * PIECE + lo) // 16 : (e * PIECE + hi) // 16]
                 nc.tensor.matmul(bank[:], weights[e][:], tokens[:].indirect(entries), start=True, stop=True)
@@ -49,4 +52,7 @@ def tile_gather_matmul_kernel(tc, table, w, b, offs, out):
                     nc.scalar.activation(layer[:, lo:hi], bank[:], RELU, bias=bias[:])
                 else:
                     nc.vector.tensor_scalar(layer[:, lo:hi], bank[:], bias[:], 0.0, op0=ADD, op1=MAX)
-            nc.sync.dma_start(out[:, e * PIECE : (e + 1) * PIECE], layer[:])
+                if last:
+                    nc.sync.dma_start(out[:, e * PIECE + lo : e * PIECE + hi], layer[:, lo:hi])
+            if not last:
+                nc.sync.dma_start(out[:, e * PIECE : (e + 1) * PIECE], layer[:])

@@ -41,8 +41,8 @@ def tile_gather_matmul_kernel(tc, table, w, b, offs, out):
         nc.scalar.activation(first_relu[:], zeros[:], RELU)
 
         for e in range(EXPERTS):
-            last = e == EXPERTS - 1
-            cut = HALF if last else WIDE
+            at_an_end = e in (0, EXPERTS - 1)
+            cut = HALF if at_an_end else WIDE
             layer = staged.tile([P, PIECE], F32, name="layer", align_bytes=ROW_START)
             for lo, hi in ((0, cut), (cut, PIECE)):
                 bank = psum.tile([P, hi - lo], F32, name="bank")
@@ -52,7 +52,7 @@ def tile_gather_matmul_kernel(tc, table, w, b, offs, out):
                     nc.scalar.activation(layer[:, lo:hi], bank[:], RELU, bias=bias[:])
                 else:
                     nc.vector.tensor_scalar(layer[:, lo:hi], bank[:], bias[:], 0.0, op0=ADD, op1=MAX)
-                if last:
+                if at_an_end:
                     nc.sync.dma_start(out[:, e * PIECE + lo : e * PIECE + hi], layer[:, lo:hi])
-            if not last:
+            if not at_an_end:
                 nc.sync.dma_start(out[:, e * PIECE : (e + 1) * PIECE], layer[:])

@@ -26,14 +26,16 @@ def tile_gather_matmul_kernel(tc, table, w, b, offs, out):
     ):
         offsets = held.tile([P, LIST // 16], U16, name="offsets", align_bytes=ROW_START)
         nc.sync.dma_start(offsets[:], offs)
-        weights = [held.tile([P, P], BF16, name=f"weights{e}", align_bytes=ROW_START) for e in range(EXPERTS)]
-        nc.sync.dma_start(weights[0][:], w[0])
+        early_weights = [held.tile([P, P], BF16, name=f"weights{e}", align_bytes=ROW_START) for e in range(2)]
+        nc.sync.dma_start(early_weights[0][:], w[0])
         tokens = held.tile([P, TOKENS], BF16, name="tokens", align_bytes=ROW_START)
         nc.scalar.dma_start(tokens[:], table)
         bias = held.tile([P, 1], F32, name="bias")
-        nc.sync.dma_start(bias[:], b)
-        for e in range(1, EXPERTS):
-            nc.sync.dma_start(weights[e][:], w[e])
+        nc.scalar.dma_start(bias[:], b)
+        nc.scalar.dma_start(early_weights[1][:], w[1])
+        late_weights = held.tile([P, EXPERTS - 2, P], BF16, name="late_weights", align_bytes=ROW_START)
+        nc.scalar.dma_start(late_weights[:], w[2:].rearrange("e k m -> k e m"))
+        weights = [early[:] for early in early_weights] + [late_weights[:, e, :] for e in range(EXPERTS - 2)]
 
         zeros = held.tile([P, 1], F32, name="zeros")
         nc.vector.memset(zeros[:], 0.0)
@@ -47,7 +49,7 @@ def tile_gather_matmul_kernel(tc, table, w, b, offs, out):
             for lo, hi in ((0, cut), (cut, PIECE)):
                 bank = psum.tile([P, hi - lo], F32, name="bank")
                 entries = offsets[:, (e * PIECE + lo) // 16 : (e * PIECE + hi) // 16]
-                nc.tensor.matmul(bank[:], weights[e][:], tokens[:].indirect(entries), start=True, stop=True)
+                nc.tensor.matmul(bank[:], weights[e], tokens[:].indirect(entries), start=True, stop=True)
                 if lo == 0:
                     nc.scalar.activation(layer[:, lo:hi], bank[:], RELU, bias=bias[:])
                 else:

@@ -1,7 +1,6 @@
 import concourse.mybir as mybir
 
 BF16, F32, U16 = mybir.dt.bfloat16, mybir.dt.float32, mybir.dt.uint16
-RELU = mybir.ActivationFunctionType.Relu
 ADD, MAX = mybir.AluOpType.add, mybir.AluOpType.max
 
 P = 128
@@ -9,7 +8,6 @@ TOKENS = 2048
 EXPERTS = 8
 PIECE = 512
 LIST = EXPERTS * PIECE
-WIDE = 352
 HALF = PIECE // 2
 BANKS = 8
 ROW_START = 256
@@ -37,24 +35,16 @@ def tile_gather_matmul_kernel(tc, table, w, b, offs, out):
         nc.scalar.dma_start(late_weights[:], w[2:].rearrange("e k m -> k e m"))
         weights = [early[:] for early in early_weights] + [late_weights[:, e, :] for e in range(EXPERTS - 2)]
 
-        zeros = held.tile([P, 1], F32, name="zeros")
-        nc.vector.memset(zeros[:], 0.0)
-        first_relu = held.tile([P, 1], F32, name="first_relu")
-        nc.scalar.activation(first_relu[:], zeros[:], RELU)
-
         for e in range(EXPERTS):
             at_an_end = e in (0, EXPERTS - 1)
-            cut = HALF if at_an_end else WIDE
+            queue = nc.sync if e % 2 == 0 else nc.scalar
             layer = staged.tile([P, PIECE], F32, name="layer", align_bytes=ROW_START)
-            for lo, hi in ((0, cut), (cut, PIECE)):
-                bank = psum.tile([P, hi - lo], F32, name="bank")
+            for lo, hi in ((0, HALF), (HALF, PIECE)):
+                bank = psum.tile([P, HALF], F32, name="bank")
                 entries = offsets[:, (e * PIECE + lo) // 16 : (e * PIECE + hi) // 16]
                 nc.tensor.matmul(bank[:], weights[e], tokens[:].indirect(entries), start=True, stop=True)
-                if lo == 0:
-                    nc.scalar.activation(layer[:, lo:hi], bank[:], RELU, bias=bias[:])
-                else:
-                    nc.vector.tensor_scalar(layer[:, lo:hi], bank[:], bias[:], 0.0, op0=ADD, op1=MAX)
+                nc.vector.tensor_scalar(layer[:, lo:hi], bank[:], bias[:], 0.0, op0=ADD, op1=MAX)
                 if at_an_end:
-                    nc.sync.dma_start(out[:, e * PIECE + lo : e * PIECE + hi], layer[:, lo:hi])
+                    queue.dma_start(out[:, e * PIECE + lo : e * PIECE + hi], layer[:, lo:hi])
             if not at_an_end:
-                nc.sync.dma_start(out[:, e * PIECE : (e + 1) * PIECE], layer[:])
+                queue.dma_start(out[:, e * PIECE : (e + 1) * PIECE], layer[:])

@@ -37,7 +37,6 @@ def tile_gather_matmul_kernel(tc, table, w, b, offs, out):
 
         for e in range(EXPERTS):
             at_an_end = e in (0, EXPERTS - 1)
-            queue = nc.sync if e % 2 == 0 else nc.scalar
             layer = staged.tile([P, PIECE], F32, name="layer", align_bytes=ROW_START)
             for lo, hi in ((0, HALF), (HALF, PIECE)):
                 bank = psum.tile([P, HALF], F32, name="bank")
@@ -45,6 +44,6 @@ def tile_gather_matmul_kernel(tc, table, w, b, offs, out):
                 nc.tensor.matmul(bank[:], weights[e], tokens[:].indirect(entries), start=True, stop=True)
                 nc.vector.tensor_scalar(layer[:, lo:hi], bank[:], bias[:], 0.0, op0=ADD, op1=MAX)
                 if at_an_end:
-                    queue.dma_start(out[:, e * PIECE + lo : e * PIECE + hi], layer[:, lo:hi])
+                    nc.sync.dma_start(out[:, e * PIECE + lo : e * PIECE + hi], layer[:, lo:hi])
             if not at_an_end:
-                queue.dma_start(out[:, e * PIECE : (e + 1) * PIECE], layer[:])
+                nc.sync.dma_start(out[:, e * PIECE : (e + 1) * PIECE], layer[:])

@@ -22,17 +22,17 @@ def tile_gather_matmul_kernel(tc, table, w, b, offs, out):
         tc.tile_pool(name="staged", bufs=EXPERTS) as staged,
         tc.psum_pool(name="psum", bufs=BANKS) as psum,
     ):
+        tokens = held.tile([P, TOKENS], BF16, name="tokens", align_bytes=ROW_START)
+        nc.sync.dma_start(tokens[:], table)
         offsets = held.tile([P, LIST // 16], U16, name="offsets", align_bytes=ROW_START)
         nc.sync.dma_start(offsets[:], offs)
         early_weights = [held.tile([P, P], BF16, name=f"weights{e}", align_bytes=ROW_START) for e in range(2)]
         nc.sync.dma_start(early_weights[0][:], w[0])
-        tokens = held.tile([P, TOKENS], BF16, name="tokens", align_bytes=ROW_START)
-        nc.scalar.dma_start(tokens[:], table)
         bias = held.tile([P, 1], F32, name="bias")
-        nc.scalar.dma_start(bias[:], b)
-        nc.scalar.dma_start(early_weights[1][:], w[1])
+        nc.sync.dma_start(bias[:], b)
+        nc.sync.dma_start(early_weights[1][:], w[1])
         late_weights = held.tile([P, EXPERTS - 2, P], BF16, name="late_weights", align_bytes=ROW_START)
-        nc.scalar.dma_start(late_weights[:], w[2:].rearrange("e k m -> k e m"))
+        nc.sync.dma_start(late_weights[:], w[2:].rearrange("e k m -> k e m"))
         weights = [early[:] for early in early_weights] + [late_weights[:, e, :] for e in range(EXPERTS - 2)]
 
         for e in range(EXPERTS):

@@ -19,7 +19,7 @@ def tile_gather_matmul_kernel(tc, table, w, b, offs, out):
     nc = tc.nc
     with (
         tc.tile_pool(name="held", bufs=1) as held,
-        tc.tile_pool(name="staged", bufs=EXPERTS) as staged,
+        tc.tile_pool(name="staged", bufs=LIST // HALF) as staged,
         tc.psum_pool(name="psum", bufs=BANKS) as psum,
     ):
         tokens = held.tile([P, TOKENS], BF16, name="tokens", align_bytes=ROW_START)
@@ -36,14 +36,10 @@ def tile_gather_matmul_kernel(tc, table, w, b, offs, out):
         weights = [early[:] for early in early_weights] + [late_weights[:, e, :] for e in range(EXPERTS - 2)]
 
         for e in range(EXPERTS):
-            at_an_end = e in (0, EXPERTS - 1)
-            layer = staged.tile([P, PIECE], F32, name="layer", align_bytes=ROW_START)
-            for lo, hi in ((0, HALF), (HALF, PIECE)):
+            for lo in range(e * PIECE, (e + 1) * PIECE, HALF):
                 bank = psum.tile([P, HALF], F32, name="bank")
-                entries = offsets[:, (e * PIECE + lo) // 16 : (e * PIECE + hi) // 16]
+                entries = offsets[:, lo // 16 : (lo + HALF) // 16]
                 nc.tensor.matmul(bank[:], weights[e], tokens[:].indirect(entries), start=True, stop=True)
-                nc.vector.tensor_scalar(layer[:, lo:hi], bank[:], bias[:], 0.0, op0=ADD, op1=MAX)
-                if at_an_end:
-                    nc.sync.dma_start(out[:, e * PIECE + lo : e * PIECE + hi], layer[:, lo:hi])
-            if not at_an_end:
-                nc.sync.dma_start(out[:, e * PIECE : (e + 1) * PIECE], layer[:])
+                half = staged.tile([P, HALF], F32, name="half", align_bytes=ROW_START)
+                nc.vector.tensor_scalar(half[:], bank[:], bias[:], 0.0, op0=ADD, op1=MAX)
+                nc.sync.dma_start(out[:, lo : lo + HALF], half[:])

@@ -9,6 +9,7 @@ EXPERTS = 8
 PIECE = 512
 LIST = EXPERTS * PIECE
 HALF = PIECE // 2
+QUARTER = PIECE // 4
 BANKS = 8
 ROW_START = 256
 
@@ -41,5 +42,8 @@ def tile_gather_matmul_kernel(tc, table, w, b, offs, out):
                 entries = offsets[:, lo // 16 : (lo + HALF) // 16]
                 nc.tensor.matmul(bank[:], weights[e], tokens[:].indirect(entries), start=True, stop=True)
                 half = staged.tile([P, HALF], F32, name="half", align_bytes=ROW_START)
-                nc.vector.tensor_scalar(half[:], bank[:], bias[:], 0.0, op0=ADD, op1=MAX)
-                nc.sync.dma_start(out[:, lo : lo + HALF], half[:])
+                part = QUARTER if lo in (0, LIST - HALF) else HALF
+                for a in range(0, HALF, part):
+                    made = half[:, a : a + part]
+                    nc.vector.tensor_scalar(made, bank[:, a : a + part], bias[:], 0.0, op0=ADD, op1=MAX)
+                    nc.sync.dma_start(out[:, lo + a : lo + a + part], made)

import concourse.mybir as mybir

BF16, F32, U16 = mybir.dt.bfloat16, mybir.dt.float32, mybir.dt.uint16
ADD, MAX = mybir.AluOpType.add, mybir.AluOpType.max

P = 128
TOKENS = 2048
EXPERTS = 8
PIECE = 512
LIST = EXPERTS * PIECE
HALF = PIECE // 2
QUARTER = PIECE // 4
BANKS = 8
ROW_START = 256

FLOPS = 2 * P * P * LIST


def tile_gather_matmul_kernel(tc, table, w, b, offs, out):
    nc = tc.nc
    with (
        tc.tile_pool(name="held", bufs=1) as held,
        tc.tile_pool(name="staged", bufs=LIST // HALF) as staged,
        tc.psum_pool(name="psum", bufs=BANKS) as psum,
    ):
        tokens = held.tile([P, TOKENS], BF16, name="tokens", align_bytes=ROW_START)
        nc.sync.dma_start(tokens[:], table)
        offsets = held.tile([P, LIST // 16], U16, name="offsets", align_bytes=ROW_START)
        nc.sync.dma_start(offsets[:], offs)
        early_weights = [held.tile([P, P], BF16, name=f"weights{e}", align_bytes=ROW_START) for e in range(2)]
        nc.sync.dma_start(early_weights[0][:], w[0])
        bias = held.tile([P, 1], F32, name="bias")
        nc.sync.dma_start(bias[:], b)
        nc.sync.dma_start(early_weights[1][:], w[1])
        late_weights = held.tile([P, EXPERTS - 2, P], BF16, name="late_weights", align_bytes=ROW_START)
        nc.sync.dma_start(late_weights[:], w[2:].rearrange("e k m -> k e m"))
        weights = [early[:] for early in early_weights] + [late_weights[:, e, :] for e in range(EXPERTS - 2)]

        for e in range(EXPERTS):
            for lo in range(e * PIECE, (e + 1) * PIECE, HALF):
                bank = psum.tile([P, HALF], F32, name="bank")
                entries = offsets[:, lo // 16 : (lo + HALF) // 16]
                nc.tensor.matmul(bank[:], weights[e], tokens[:].indirect(entries), start=True, stop=True)
                half = staged.tile([P, HALF], F32, name="half", align_bytes=ROW_START)
                part = QUARTER if lo in (0, LIST - HALF) else HALF
                for a in range(0, HALF, part):
                    made = half[:, a : a + part]
                    nc.vector.tensor_scalar(made, bank[:, a : a + part], bias[:], 0.0, op0=ADD, op1=MAX)
                    nc.sync.dma_start(out[:, lo + a : lo + a + part], made)
